import numpy as np
import ml_dtypes


def mxq(x, axis, fmt="e4m3"):
    dtype, down = {"e4m3": (ml_dtypes.float8_e4m3fn, 7), "e5m2": (ml_dtypes.float8_e5m2, 14)}[fmt]
    v = np.moveaxis(np.asarray(x, np.float32).astype(ml_dtypes.bfloat16).astype(np.float64), axis, -1)
    blocks = v.reshape(v.shape[:-1] + (-1, 32))
    amax = np.abs(blocks).max(-1, keepdims=True)
    byte = np.maximum(np.where(amax > 0, np.frexp(amax)[1] - 1 + 127, 0) - down, 1)
    scale = np.exp2(byte - 127.0)
    codes = (blocks / scale).astype(np.float32).astype(dtype).astype(np.float64)
    return np.moveaxis((codes * scale).reshape(v.shape), -1, axis)


WIDE = False


def mx_kscale(k):
    if not WIDE:
        return np.ones(k)
    levels = np.array([10, -10, 5, -5, 0])
    if k % 512:
        return np.exp2(np.random.permutation(np.resize(levels, k // 32))).repeat(32)
    a = np.empty((k // 512, 16))
    for p in range(k // 512):
        a[p, :8] = np.random.permutation(np.resize(levels, 8))
        for g in range(8):
            far = levels[np.abs(levels - a[p, g]) >= 10]
            a[p, g + 8] = far[np.random.randint(len(far))]
    return np.exp2(a.ravel()).repeat(32)


BF16 = ml_dtypes.bfloat16


def bf(x):
    return np.asarray(x, np.float32).astype(BF16)


def f64(x):
    return np.asarray(x).astype(np.float64)

def planes(Y):
    n, m = Y.shape
    b = f64(bf(Y)).reshape(n // 32, 32, m)
    amax = np.abs(b).max(1)
    byte = np.clip(np.where(amax > 0, np.frexp(amax)[1] - 1 + 127 - 7, 1), 1, 254)
    codes = (b * np.exp2(127.0 - byte)[:, None, :]).reshape(n, m).astype(np.float32).astype(ml_dtypes.float8_e4m3fn).view(np.uint8)
    words = codes.reshape(n // 512, 128, 4, m).transpose(0, 1, 3, 2)
    return np.ascontiguousarray(words), np.ascontiguousarray(byte.astype(np.uint8).reshape(n // 512, 16, m))


B, N, R, W = 4, 512, 256, 512


def update_link(link, w, p):
    w_row = w[:, :, None]
    w_col = w[:, None, :]
    l2 = (1.0 - w_row - w_col) * link + w_row * p[:, None, :]
    idx = np.arange(link.shape[-1])
    on_diag = idx[:, None] == idx[None, :]
    return np.where(on_diag[None, :, :], 0.0, l2)


def setup_inputs():
    s, t = mx_kscale(N), mx_kscale(N)
    return {"link": bf(np.random.standard_normal((B, N, N)) / np.sqrt(N)),
            "w": bf(np.random.uniform(0.0, 0.5, (B, N))),
            "p": bf(np.random.standard_normal((B, N)) * 2.25 / np.sqrt(N)),
            "r": bf(np.random.standard_normal((B, R, N)) * s),
            "g": bf((1.0 + 0.1 * np.random.standard_normal(N)) / s),
            "h": bf((1.0 + 0.1 * np.random.standard_normal(N)) * t),
            "m": bf(np.random.standard_normal((B, N, W)) / np.sqrt(N) / t[:, None])}


def core(link, w, p, r, g, h, m):
    l2 = update_link(f64(link), f64(w), f64(p))
    g, h = f64(g), f64(h)
    rq = mxq(f64(r), 2, "e4m3")
    lf = mxq(l2 * g[None, None, :], 2, "e4m3")
    fw = rq @ lf.transpose(0, 2, 1)
    lb = mxq(l2 * g[None, :, None], 1, "e4m3")
    bw = rq @ lb
    a = (0.7 * fw + 0.3 * bw) * h[None, None, :]
    return mxq(a, 2, "e4m3") @ mxq(f64(m), 1, "e4m3")


def reference(link, w, p, r, g, h, m):
    R_out = core(link, w, p, r, g, h, m)
    words, scales = planes(np.moveaxis(R_out, 2, 0).reshape(512, -1))
    return R_out, words, scales

@@ -1,0 +1,347 @@
+from contextlib import ExitStack
+
+import concourse.mybir as mybir
+from concourse.masks import make_identity
+
+FLOPS = 4 * 3 * 2 * 256 * 512 * 512
+
+F32 = mybir.dt.float32
+BF16 = mybir.dt.bfloat16
+U32 = mybir.dt.uint32
+I32 = mybir.dt.int32
+U8 = mybir.dt.uint8
+FP8X4 = mybir.dt.float8_e4m3fn_x4
+ADD = mybir.AluOpType.add
+SUB = mybir.AluOpType.subtract
+MULT = mybir.AluOpType.mult
+COPY = mybir.ActivationFunctionType.Copy
+
+B, N, R, W = 4, 512, 256, 512
+P = 128
+
+
+def tile_dnctemporallinkreadout_x1_kernel(tc, link, w, p, r, g, h, m, out_0, out_1, out_2):
+    nc = tc.nc
+    with ExitStack() as ctx:
+        ctx.enter_context(tc.manual_schedule())
+        const = ctx.enter_context(tc.tile_pool(name="const", bufs=1))
+        raw = ctx.enter_context(tc.tile_pool(name="raw", bufs=4))
+        work = ctx.enter_context(tc.tile_pool(name="work", bufs=2))
+        ps_bc = ctx.enter_context(tc.psum_pool(name="ps_bc", bufs=1))
+        ps_tr = ctx.enter_context(tc.psum_pool(name="ps_tr", bufs=3))
+        ps_s1 = ctx.enter_context(tc.psum_pool(name="ps_s1", bufs=2))
+        ps_s2 = ctx.enter_context(tc.psum_pool(name="ps_s2", bufs=2))
+
+        w_ps = const.tile([P, B, 4], BF16, name="w_ps", align_bytes=64)
+        p_ps = const.tile([P, B, 4], BF16, name="p_ps", align_bytes=64)
+        g_ps = const.tile([P, 4], BF16, name="g_ps", align_bytes=64)
+        h_ps = const.tile([P, 4], BF16, name="h_ps", align_bytes=64)
+        linkt, rt, mt = {}, {}, {}
+
+        def load_link(b, s0, parts):
+            lv = link[b].rearrange("(p s) q -> p s q", s=4)
+            for n in parts:
+                if n == 4:
+                    t = raw.tile([P, n, N], BF16, name="link_all", align_bytes=64)
+                else:
+                    t = const.tile([P, n, N], BF16, name=f"link_first_{s0}", align_bytes=64)
+                nc.sync.dma_start(out=t[:], in_=lv[:, s0:s0 + n, :])
+                for j in range(n):
+                    linkt[b, s0 + j] = t[:, j, :]
+                s0 += n
+
+        def load_r(b):
+            t = raw.tile([P, 2, N], BF16, name="r_raw", align_bytes=64)
+            nc.sync.dma_start(out=t[:], in_=r[b].rearrange("(c k) j -> k c j", k=P))
+            rt[b] = t
+
+        def load_m(b):
+            t = raw.tile([P, 4, W], BF16, name="m_raw", align_bytes=64)
+            nc.sync.dma_start(out=t[:], in_=m[b].rearrange("(p j) c -> p j c", j=4))
+            mt[b] = t
+
+        with nc.allow_non_contiguous_dma(reason="8-byte pieces of the small vectors"):
+            nc.scalar.dma_start(out=w_ps[:], in_=w.rearrange("b (p s) -> p b s", s=4))
+            load_link(0, 0, (1,))
+            nc.scalar.dma_start(out=p_ps[:], in_=p.rearrange("b (p s) -> p b s", s=4))
+            nc.scalar.dma_start(out=g_ps[:], in_=g.rearrange("(p s) -> p s", s=4))
+            nc.scalar.dma_start(out=h_ps[:], in_=h.rearrange("(p s) -> p s", s=4))
+        load_link(0, 1, (1, 2))
+        load_r(0)
+        load_link(1, 0, (4,))
+        load_m(0)
+        load_r(1)
+        load_link(2, 0, (4,))
+        load_m(1)
+        load_r(2)
+        load_link(3, 0, (4,))
+        load_r(3)
+        load_m(2)
+        load_m(3)
+
+        ident_b = const.tile([P, P], BF16, name="ident_b", align_bytes=64)
+        ident_f = const.tile([P, P], F32, name="ident_f", align_bytes=64)
+        make_identity(nc, ident_b[:])
+        make_identity(nc, ident_f[:])
+        gmask = const.tile([P, N, 4], BF16, name="gmask", align_bytes=64)
+        nc.scalar.copy(out=gmask[:], in_=g_ps[:].unsqueeze(1).to_broadcast([P, N, 4]))
+        nc.gpsimd.affine_select(
+            out=gmask[:].rearrange("p c s -> p (c s)"), in_=gmask[:].rearrange("p c s -> p (c s)"),
+            pattern=[[1, 4], [4, P], [-1, 4]], compare_op=mybir.AluOpType.not_equal,
+            fill=0.0, base=0, channel_multiplier=-4)
+        wm1 = const.tile([P, B, 4], F32, name="wm1", align_bytes=64)
+        nc.vector.tensor_scalar(out=wm1[:], in0=w_ps[:], scalar1=-1.0, scalar2=None, op0=ADD)
+        h07 = const.tile([P, 4], F32, name="h07", align_bytes=64)
+        h03 = const.tile([P, 4], F32, name="h03", align_bytes=64)
+
+        p_codes = const.tile([P, B * R], U32, name="p_codes", align_bytes=64)
+        p_scales = const.tile([P, B * R], U8, name="p_scales", align_bytes=64)
+
+        bc, tr = {}, {}
+        U, Q, lfI, lbI, lfC, lfS, lbC, lbS = {}, {}, {}, {}, {}, {}, {}, {}
+        rI, rC, rS, mI, mC, mS = {}, {}, {}, {}, {}, {}
+        fwS, bwS, aI, aC, aS, pI, oS = {}, {}, {}, {}, {}, {}, {}
+
+        def bcast(b):
+            bc[b] = ps_bc.tile([P, 2, N], BF16, name="bc")
+            for i, v in enumerate((w_ps, p_ps)):
+                for t in range(4):
+                    nc.tensor.transpose(bc[b][:, i, t * P:(t + 1) * P],
+                                        v[:, b, t:t + 1].to_broadcast([P, P]), ident_b[:])
+
+        def r_trans(b):
+            t = ps_tr.tile([P, 2, 2, P], F32, name="tr_r", tag="tr")
+            for c in range(2):
+                words = rt[b][:, c, :].bitcast(F32)
+                for u in range(2):
+                    nc.tensor.transpose(t[:, c, u, :], words[:, u:2 * P:2], ident_f[:])
+            rI[b] = work.tile([P, R, 4], BF16, name="rI", align_bytes=64)
+            nc.scalar.copy(
+                out=rI[b][:].rearrange("p k t -> p (k t)").bitcast(F32).rearrange("p (c k u) -> p c k u", c=2, u=2),
+                in_=t[:].rearrange("p c u k -> p c k u"))
+
+        def quant(src, cols, codes, scales):
+            nc.vector.quantize_mx(out=codes.bitcast(FP8X4), scales=scales, in_=src)
+
+        def q_tile(store_c, store_s, b, src, cols, nm, n0=0, n1=None):
+            n1 = cols if n1 is None else n1
+            if n0 == 0:
+                store_c[b] = work.tile([P, cols], U32, name=nm + "C", align_bytes=64)
+                store_s[b] = work.tile([P, cols], U8, name=nm + "S", align_bytes=64)
+            quant(src[b][:, n0:n1, :].rearrange("p c s -> p (c s)"), cols, store_c[b][:, n0:n1], store_s[b][:, n0:n1])
+
+        def v1(b, s):
+            if s == 0:
+                Q[b] = work.tile([P, 4, N], F32, name="Q", align_bytes=64)
+            U[b, s] = work.tile([P, N], F32, name="U", bufs=4, align_bytes=64)
+            nc.vector.scalar_tensor_tensor(
+                out=U[b, s][:].rearrange("p (u m) -> p u m", u=4),
+                in0=bc[b][:, 0, :].rearrange("p (u m) -> p u m", u=4), scalar=wm1[:, b, s:s + 1],
+                in1=linkt[b, s].rearrange("p (m u) -> p u m", u=4), op0=ADD, op1=MULT)
+
+        def v2(b, s):
+            nc.vector.scalar_tensor_tensor(
+                out=Q[b][:, s, :], in0=bc[b][:, 1, :], scalar=w_ps[:, b, s:s + 1],
+                in1=U[b, s][:], op0=MULT, op1=SUB)
+
+        def tq(b, s):
+            tr[b, s] = ps_tr.tile([P, 4, P], F32, name="tr_q", tag="tr")
+            for u in range(4):
+                nc.tensor.transpose(tr[b, s][:, u, :], Q[b][:, s, u * P:(u + 1) * P], ident_f[:])
+
+        def v4(b, s):
+            if s == 0:
+                lfI[b] = work.tile([P, N, 4], BF16, name="lfI", align_bytes=64)
+            nc.vector.tensor_tensor(
+                out=lfI[b][:, s * P:(s + 1) * P, :], in0=tr[b, s][:].rearrange("p u n -> p n u"),
+                in1=gmask[:, s * P:(s + 1) * P, :], op=MULT)
+
+        def lb(b, eng, c0, c1):
+            if c0 == 0:
+                lbI[b] = work.tile([P, N, 4], BF16, name="lbI", align_bytes=64)
+            eng.tensor_tensor(
+                out=lbI[b][:, c0:c1, :], in0=Q[b][:, :, c0:c1].rearrange("p s c -> p c s"),
+                in1=gmask[:, c0:c1, :], op=MULT)
+
+        def m_copy(b):
+            mI[b] = work.tile([P, W, 4], BF16, name="mI", align_bytes=64)
+            nc.scalar.copy(out=mI[b][:].rearrange("p (t m) j -> p t m j", t=4),
+                           in_=mt[b][:].rearrange("p j (m t) -> p t m j", t=4))
+
+        def exit1(b, acc, dst, hs, eng, half):
+            for i in range(2):
+                t = 2 * half + i
+                if eng == "V":
+                    nc.vector.tensor_scalar(out=dst[b][:, t, :], in0=acc[:, i, :], scalar1=hs[:, t:t + 1],
+                                            scalar2=None, op0=MULT)
+                else:
+                    nc.scalar.activation(out=dst[b][:, t, :], in_=acc[:, i, :], func=COPY, scale=hs[:, t:t + 1])
+
+        def stage1(b, codes, scales, dst, hs, nm, engs="SS"):
+            dst[b] = work.tile([P, 4, R], F32, name=nm, align_bytes=64)
+            todo = []
+            for half in range(2):
+                acc = ps_s1.tile([P, 2, R], F32, name="s1")
+                for i in range(2):
+                    t = 2 * half + i
+                    nc.tensor.matmul_mx(
+                        out=acc[:, i, :], lhsT=codes[b][:, t * P:(t + 1) * P].bitcast(FP8X4),
+                        lhsT_scale=scales[b][:, t * P:(t + 1) * P],
+                        rhs=rC[b][:].bitcast(FP8X4), rhs_scale=rS[b][:], start=True, stop=True)
+                if engs[half] == "S":
+                    exit1(b, acc, dst, hs, "S", half)
+                else:
+                    todo.append((b, acc, dst, hs, "V", half))
+            return todo
+
+        def a_add(b, c):
+            if c == 0:
+                aI[b] = work.tile([P, R, 4], BF16, name="aI", align_bytes=64)
+            ks = slice(c * P, (c + 1) * P)
+            nc.vector.tensor_tensor(
+                out=aI[b][:, ks, :], in0=fwS[b][:, :, ks].rearrange("p t k -> p k t"),
+                in1=bwS[b][:, :, ks].rearrange("p t k -> p k t"), op=ADD)
+
+        def p_mm(b, c):
+            if c == 0:
+                pI[b] = work.tile([P, R, 4], BF16, name="pI", align_bytes=64)
+            ks = slice(c * P, (c + 1) * P)
+            pp = ps_s2.tile([P, 4, P], F32, name="pp", tag="s2")
+            for t in range(4):
+                nc.tensor.matmul_mx(
+                    out=pp[:, t, :], lhsT=mC[b][:, t * P:(t + 1) * P].bitcast(FP8X4),
+                    lhsT_scale=mS[b][:, t * P:(t + 1) * P],
+                    rhs=aC[b][:, ks].bitcast(FP8X4), rhs_scale=aS[b][:, ks], start=True, stop=True)
+            return pp
+
+        def p_exit(b, c, pp, eng):
+            ks = slice(c * P, (c + 1) * P)
+            if eng == "V":
+                nc.vector.tensor_copy(out=pI[b][:, ks, :], in_=pp[:].rearrange("p t k -> p k t"))
+            else:
+                nc.scalar.copy(out=pI[b][:, ks, :], in_=pp[:].rearrange("p t k -> p k t"))
+
+        def o_mm(b, c):
+            if c == 0:
+                oS[b] = work.tile([P, 2, W], F32, name="oS", align_bytes=64)
+            ks = slice(c * P, (c + 1) * P)
+            oo = ps_s2.tile([P, W], F32, name="oo", tag="s2")
+            nc.tensor.matmul_mx(
+                out=oo[:], lhsT=aC[b][:, ks].bitcast(FP8X4), lhsT_scale=aS[b][:, ks],
+                rhs=mC[b][:].bitcast(FP8X4), rhs_scale=mS[b][:], start=True, stop=True)
+            return oo
+
+        def o_exit(b, c, oo, eng):
+            dst = oS[b][:, c, :].rearrange("p (m t) -> p m t", t=4)
+            src = oo[:].rearrange("p (t m) -> p m t", t=4)
+            if eng == "V":
+                nc.vector.tensor_copy(out=dst, in_=src)
+            else:
+                nc.scalar.copy(out=dst, in_=src)
+
+        def o_store(b, c0, c1):
+            nc.sync.dma_start(out=out_0[b].rearrange("(c k) n -> k c n", k=P)[:, c0:c1, :], in_=oS[b][:, c0:c1, :])
+
+        def q_p(b, c0, c1):
+            ms = slice(b * R + c0 * P, b * R + c1 * P)
+            quant(pI[b][:, c0 * P:c1 * P, :].rearrange("p c s -> p (c s)"), R, p_codes[:, ms], p_scales[:, ms])
+            nc.sync.dma_start(out=out_1[0, :, ms, :].rearrange("p k t -> p (k t)").bitcast(I32),
+                              in_=p_codes[:, ms].bitcast(I32))
+
+        def scale_store(b0, b1):
+            ms = slice(b0 * R, b1 * R)
+            for q in range(4):
+                nc.sync.dma_start(out=out_2[0, 4 * q:4 * q + 4, ms].bitcast(I32),
+                                  in_=p_scales[32 * q:32 * q + 4, ms].bitcast(I32))
+
+        def stage2(b):
+            for c in range(2):
+                p_exit(b, c, p_mm(b, c), "S")
+            for c in range(2):
+                o_exit(b, c, o_mm(b, c), "S")
+            o_store(b, 0, 2)
+
+        bcast(0)
+        HALF = 256
+        LAST = 288
+        for i in range(B):
+            prev, end = i > 0, i == B - 1
+            v1(i, 0)
+            if i == 0:
+                nc.vector.tensor_scalar(out=h07[:], in0=h_ps[:], scalar1=0.7, scalar2=None, op0=MULT)
+                nc.vector.tensor_scalar(out=h03[:], in0=h_ps[:], scalar1=0.3, scalar2=None, op0=MULT)
+            if prev:
+                lb(i - 1, nc.gpsimd, HALF, N)
+                m_copy(i - 1)
+            v1(i, 1)
+            v2(i, 0)
+            tq(i, 0)
+            v1(i, 2)
+            v2(i, 1)
+            tq(i, 1)
+            v1(i, 3)
+            v2(i, 2)
+            if i == 0:
+                r_trans(0)
+            else:
+                tq(i, 2)
+            if prev:
+                q_tile(lbC, lbS, i - 1, lbI, N, "lb")
+                stage1(i - 1, lbC, lbS, bwS, h03, "bwS")
+            v2(i, 3)
+            lb(i, nc.gpsimd, 0, LAST if end else HALF)
+            if end:
+                m_copy(i)
+            v4(i, 0)
+            if i == 0:
+                tq(i, 2)
+            v4(i, 1)
+            tq(i, 3)
+            if not end:
+                bcast(i + 1)
+            v4(i, 2)
+            v4(i, 3)
+            if end:
+                lb(i, nc.vector, LAST, N)
+            q_tile(rC, rS, i, rI, R, "r")
+            q_tile(lfC, lfS, i, lfI, N, "lf")
+            stage1(i, lfC, lfS, fwS, h07, "fwS")
+            if not end:
+                r_trans(i + 1)
+            else:
+                q_tile(lbC, lbS, i, lbI, N, "lb")
+                todo = stage1(i, lbC, lbS, bwS, h03, "bwS", "SV")
+            if prev:
+                q_tile(mC, mS, i - 1, mI, W, "m")
+                a_add(i - 1, 0)
+                a_add(i - 1, 1)
+                if i > 1:
+                    q_p(i - 2, 0, 2)
+                q_tile(aC, aS, i - 1, aI, R, "a")
+                if not end:
+                    stage2(i - 1)
+        j, k = B - 1, B - 2
+        scale_store(0, k)
+        for args in todo:
+            exit1(*args)
+        p_exit(k, 0, p_mm(k, 0), "S")
+        p_exit(k, 1, p_mm(k, 1), "S")
+        q_tile(mC, mS, j, mI, W, "m")
+        a_add(j, 0)
+        a_add(j, 1)
+        q_tile(aC, aS, j, aI, R, "a", 0, P)
+        q_tile(aC, aS, j, aI, R, "a", P, R)
+        q_p(k, 0, 2)
+        pp0 = p_mm(j, 0)
+        pp1 = p_mm(j, 1)
+        p_exit(j, 0, pp0, "S")
+        p_exit(j, 1, pp1, "V")
+        o_exit(k, 0, o_mm(k, 0), "S")
+        o_exit(k, 1, o_mm(k, 1), "V")
+        o_store(k, 0, 2)
+        q_p(j, 0, 2)
+        o_exit(j, 0, o_mm(j, 0), "S")
+        o_store(j, 0, 1)
+        o_exit(j, 1, o_mm(j, 1), "V")
+        o_store(j, 1, 2)
+        scale_store(k, B)

@@ -27,13 +27,16 @@ def tile_dnctemporallinkreadout_x1_kernel(tc, link, w, p, r, g, h, m, out_0, out
         const = ctx.enter_context(tc.tile_pool(name="const", bufs=1))
         raw = ctx.enter_context(tc.tile_pool(name="raw", bufs=4))
         work = ctx.enter_context(tc.tile_pool(name="work", bufs=2))
-        ps_bc = ctx.enter_context(tc.psum_pool(name="ps_bc", bufs=1))
-        ps_tr = ctx.enter_context(tc.psum_pool(name="ps_tr", bufs=3))
+        ps_tr = ctx.enter_context(tc.psum_pool(name="ps_tr", bufs=4))
         ps_s1 = ctx.enter_context(tc.psum_pool(name="ps_s1", bufs=2))
         ps_s2 = ctx.enter_context(tc.psum_pool(name="ps_s2", bufs=2))
 
-        w_ps = const.tile([P, B, 4], BF16, name="w_ps", align_bytes=64)
-        p_ps = const.tile([P, B, 4], BF16, name="p_ps", align_bytes=64)
+        w_ps = [const.tile([P, n, 4], BF16, name=f"w_ps{n}", align_bytes=64) for n in (1, B - 1)]
+        p_ps = [const.tile([P, n, 4], BF16, name=f"p_ps{n}", align_bytes=64) for n in (1, B - 1)]
+        wm1 = [const.tile([P, n, 4], F32, name=f"wm1{n}", align_bytes=64) for n in (1, B - 1)]
+
+        def col(pair, b, s):
+            return pair[0][:, 0, s:s + 1] if b == 0 else pair[1][:, b - 1, s:s + 1]
         g_ps = const.tile([P, 4], BF16, name="g_ps", align_bytes=64)
         h_ps = const.tile([P, 4], BF16, name="h_ps", align_bytes=64)
         linkt, rt, mt = {}, {}, {}
@@ -61,12 +64,17 @@ def tile_dnctemporallinkreadout_x1_kernel(tc, link, w, p, r, g, h, m, out_0, out
             mt[b] = t
 
         with nc.allow_non_contiguous_dma(reason="8-byte pieces of the small vectors"):
-            nc.scalar.dma_start(out=w_ps[:], in_=w.rearrange("b (p s) -> p b s", s=4))
+            wv = w.rearrange("b (p s) -> p b s", s=4)
+            pv = p.rearrange("b (p s) -> p b s", s=4)
+            nc.scalar.dma_start(out=w_ps[0][:], in_=wv[:, 0:1, :])
             load_link(0, 0, (1,))
-            nc.scalar.dma_start(out=p_ps[:], in_=p.rearrange("b (p s) -> p b s", s=4))
+            nc.scalar.dma_start(out=p_ps[0][:], in_=pv[:, 0:1, :])
+            load_link(0, 1, (1,))
             nc.scalar.dma_start(out=g_ps[:], in_=g.rearrange("(p s) -> p s", s=4))
+            load_link(0, 2, (2,))
+            nc.scalar.dma_start(out=w_ps[1][:], in_=wv[:, 1:B, :])
+            nc.scalar.dma_start(out=p_ps[1][:], in_=pv[:, 1:B, :])
             nc.scalar.dma_start(out=h_ps[:], in_=h.rearrange("(p s) -> p s", s=4))
-        load_link(0, 1, (1, 2))
         load_r(0)
         load_link(1, 0, (4,))
         load_m(0)
@@ -83,31 +91,25 @@ def tile_dnctemporallinkreadout_x1_kernel(tc, link, w, p, r, g, h, m, out_0, out
         ident_f = const.tile([P, P], F32, name="ident_f", align_bytes=64)
         make_identity(nc, ident_b[:])
         make_identity(nc, ident_f[:])
-        gmask = const.tile([P, N, 4], BF16, name="gmask", align_bytes=64)
-        nc.scalar.copy(out=gmask[:], in_=g_ps[:].unsqueeze(1).to_broadcast([P, N, 4]))
-        nc.gpsimd.affine_select(
-            out=gmask[:].rearrange("p c s -> p (c s)"), in_=gmask[:].rearrange("p c s -> p (c s)"),
-            pattern=[[1, 4], [4, P], [-1, 4]], compare_op=mybir.AluOpType.not_equal,
-            fill=0.0, base=0, channel_multiplier=-4)
-        wm1 = const.tile([P, B, 4], F32, name="wm1", align_bytes=64)
-        nc.vector.tensor_scalar(out=wm1[:], in0=w_ps[:], scalar1=-1.0, scalar2=None, op0=ADD)
+        nc.vector.tensor_scalar(out=wm1[0][:], in0=w_ps[0][:], scalar1=-1.0, scalar2=None, op0=ADD)
+        g32 = const.tile([P, 4], F32, name="g32", align_bytes=64)
         h07 = const.tile([P, 4], F32, name="h07", align_bytes=64)
         h03 = const.tile([P, 4], F32, name="h03", align_bytes=64)
 
         p_codes = const.tile([P, B * R], U32, name="p_codes", align_bytes=64)
         p_scales = const.tile([P, B * R], U8, name="p_scales", align_bytes=64)
 
-        bc, tr = {}, {}
+        bc, tr, lfN, lbN = {}, {}, {}, {}
         U, Q, lfI, lbI, lfC, lfS, lbC, lbS = {}, {}, {}, {}, {}, {}, {}, {}
         rI, rC, rS, mI, mC, mS = {}, {}, {}, {}, {}, {}
         fwS, bwS, aI, aC, aS, pI, oS = {}, {}, {}, {}, {}, {}, {}
 
         def bcast(b):
-            bc[b] = ps_bc.tile([P, 2, N], BF16, name="bc")
+            bc[b] = ps_tr.tile([P, 2, N], BF16, name="bc", tag="tr")
             for i, v in enumerate((w_ps, p_ps)):
                 for t in range(4):
                     nc.tensor.transpose(bc[b][:, i, t * P:(t + 1) * P],
-                                        v[:, b, t:t + 1].to_broadcast([P, P]), ident_b[:])
+                                        col(v, b, t).to_broadcast([P, P]), ident_b[:])
 
         def r_trans(b):
             t = ps_tr.tile([P, 2, 2, P], F32, name="tr_r", tag="tr")
@@ -136,32 +138,44 @@ def tile_dnctemporallinkreadout_x1_kernel(tc, link, w, p, r, g, h, m, out_0, out
             U[b, s] = work.tile([P, N], F32, name="U", bufs=4, align_bytes=64)
             nc.vector.scalar_tensor_tensor(
                 out=U[b, s][:].rearrange("p (u m) -> p u m", u=4),
-                in0=bc[b][:, 0, :].rearrange("p (u m) -> p u m", u=4), scalar=wm1[:, b, s:s + 1],
+                in0=bc[b][:, 0, :].rearrange("p (u m) -> p u m", u=4), scalar=col(wm1, b, s),
                 in1=linkt[b, s].rearrange("p (m u) -> p u m", u=4), op0=ADD, op1=MULT)
 
         def v2(b, s):
             nc.vector.scalar_tensor_tensor(
-                out=Q[b][:, s, :], in0=bc[b][:, 1, :], scalar=w_ps[:, b, s:s + 1],
+                out=Q[b][:, s, :], in0=bc[b][:, 1, :], scalar=col(w_ps, b, s),
                 in1=U[b, s][:], op0=MULT, op1=SUB)
 
-        def tq(b, s):
-            tr[b, s] = ps_tr.tile([P, 4, P], F32, name="tr_q", tag="tr")
-            for u in range(4):
-                nc.tensor.transpose(tr[b, s][:, u, :], Q[b][:, s, u * P:(u + 1) * P], ident_f[:])
+        def mask(b, s):
+            blk = Q[b][:, s, s * P:(s + 1) * P]
+            nc.gpsimd.affine_select(out=blk, in_=blk, pattern=[[-1, P]], compare_op=mybir.AluOpType.not_equal,
+                                    fill=0.0, base=0, channel_multiplier=1)
 
-        def v4(b, s):
-            if s == 0:
+        def tq(b, u):
+            tr[b, u] = ps_tr.tile([P, 4, P], F32, name="tr_q", tag="tr")
+            for s in range(4):
+                nc.tensor.transpose(tr[b, u][:, s, :], Q[b][:, s, u * P:(u + 1) * P], ident_f[:])
+
+        def lf_exit(b, u):
+            if u == 0:
+                lfN[b] = work.tile([P, 4, N], BF16, name="lfN", align_bytes=64)
                 lfI[b] = work.tile([P, N, 4], BF16, name="lfI", align_bytes=64)
-            nc.vector.tensor_tensor(
-                out=lfI[b][:, s * P:(s + 1) * P, :], in0=tr[b, s][:].rearrange("p u n -> p n u"),
-                in1=gmask[:, s * P:(s + 1) * P, :], op=MULT)
+            nc.scalar.activation(out=lfN[b][:, u, :], in_=tr[b, u][:].rearrange("p s k -> p (s k)"),
+                                 func=COPY, scale=g32[:, u:u + 1])
+
+        def interleave(dst, src, c0, c1):
+            nc.vector.tensor_copy(out=dst[:, c0:c1, :], in_=src[:, :, c0:c1].rearrange("p u c -> p c u"))
+
+        def lb_scale(b, c0, c1):
+            lbN[b] = work.tile([P, 4, N], BF16, name="lbN", align_bytes=64)
+            for s in range(4):
+                nc.scalar.activation(out=lbN[b][:, s, c0:c1], in_=Q[b][:, s, c0:c1], func=COPY, scale=g32[:, s:s + 1])
 
         def lb(b, eng, c0, c1):
-            if c0 == 0:
-                lbI[b] = work.tile([P, N, 4], BF16, name="lbI", align_bytes=64)
+            lbI[b] = work.tile([P, N, 4], BF16, name="lbI", align_bytes=64)
             eng.tensor_tensor(
                 out=lbI[b][:, c0:c1, :], in0=Q[b][:, :, c0:c1].rearrange("p s c -> p c s"),
-                in1=gmask[:, c0:c1, :], op=MULT)
+                in1=g_ps[:].unsqueeze(1).to_broadcast([P, c1 - c0, 4]), op=MULT)
 
         def m_copy(b):
             mI[b] = work.tile([P, W, 4], BF16, name="mI", align_bytes=64)
@@ -221,11 +235,12 @@ def tile_dnctemporallinkreadout_x1_kernel(tc, link, w, p, r, g, h, m, out_0, out
             else:
                 nc.scalar.copy(out=pI[b][:, ks, :], in_=pp[:].rearrange("p t k -> p k t"))
 
-        def o_mm(b, c):
+        def o_mm(b, c, early=False):
             if c == 0:
                 oS[b] = work.tile([P, 2, W], F32, name="oS", align_bytes=64)
             ks = slice(c * P, (c + 1) * P)
-            oo = ps_s2.tile([P, W], F32, name="oo", tag="s2")
+            pool, tag = (ps_tr, "tr") if early else (ps_s2, "s2")
+            oo = pool.tile([P, W], F32, name="oo", tag=tag)
             nc.tensor.matmul_mx(
                 out=oo[:], lhsT=aC[b][:, ks].bitcast(FP8X4), lhsT_scale=aS[b][:, ks],
                 rhs=mC[b][:].bitcast(FP8X4), rhs_scale=mS[b][:], start=True, stop=True)
@@ -261,87 +276,78 @@ def tile_dnctemporallinkreadout_x1_kernel(tc, link, w, p, r, g, h, m, out_0, out
                 o_exit(b, c, o_mm(b, c), "S")
             o_store(b, 0, 2)
 
+        SPLIT = 256
         bcast(0)
-        HALF = 256
-        LAST = 288
         for i in range(B):
             prev, end = i > 0, i == B - 1
             v1(i, 0)
-            if i == 0:
-                nc.vector.tensor_scalar(out=h07[:], in0=h_ps[:], scalar1=0.7, scalar2=None, op0=MULT)
-                nc.vector.tensor_scalar(out=h03[:], in0=h_ps[:], scalar1=0.3, scalar2=None, op0=MULT)
-            if prev:
-                lb(i - 1, nc.gpsimd, HALF, N)
-                m_copy(i - 1)
             v1(i, 1)
             v2(i, 0)
-            tq(i, 0)
+            mask(i, 0)
+            if prev:
+                m_copy(i)
             v1(i, 2)
             v2(i, 1)
-            tq(i, 1)
+            mask(i, 1)
             v1(i, 3)
             v2(i, 2)
+            mask(i, 2)
             if i == 0:
                 r_trans(0)
-            else:
-                tq(i, 2)
-            if prev:
-                q_tile(lbC, lbS, i - 1, lbI, N, "lb")
-                stage1(i - 1, lbC, lbS, bwS, h03, "bwS")
+                nc.vector.tensor_scalar(out=wm1[1][:], in0=w_ps[1][:], scalar1=-1.0, scalar2=None, op0=ADD)
+                nc.vector.tensor_scalar(out=g32[:], in0=g_ps[:], scalar1=1.0, scalar2=None, op0=MULT)
+                nc.vector.tensor_scalar(out=h07[:], in0=h_ps[:], scalar1=0.7, scalar2=None, op0=MULT)
+                nc.vector.tensor_scalar(out=h03[:], in0=h_ps[:], scalar1=0.3, scalar2=None, op0=MULT)
             v2(i, 3)
-            lb(i, nc.gpsimd, 0, LAST if end else HALF)
-            if end:
-                m_copy(i)
-            v4(i, 0)
-            if i == 0:
-                tq(i, 2)
-            v4(i, 1)
-            tq(i, 3)
-            if not end:
-                bcast(i + 1)
-            v4(i, 2)
-            v4(i, 3)
-            if end:
-                lb(i, nc.vector, LAST, N)
-            q_tile(rC, rS, i, rI, R, "r")
-            q_tile(lfC, lfS, i, lfI, N, "lf")
-            stage1(i, lfC, lfS, fwS, h07, "fwS")
-            if not end:
-                r_trans(i + 1)
-            else:
-                q_tile(lbC, lbS, i, lbI, N, "lb")
-                todo = stage1(i, lbC, lbS, bwS, h03, "bwS", "SV")
+            mask(i, 3)
             if prev:
-                q_tile(mC, mS, i - 1, mI, W, "m")
                 a_add(i - 1, 0)
                 a_add(i - 1, 1)
-                if i > 1:
-                    q_p(i - 2, 0, 2)
+                q_tile(mC, mS, i, mI, W, "m")
                 q_tile(aC, aS, i - 1, aI, R, "a")
-                if not end:
-                    stage2(i - 1)
-        j, k = B - 1, B - 2
-        scale_store(0, k)
+            for u in range(4):
+                tq(i, u)
+            lb_scale(i, 0, SPLIT)
+            for u in range(4):
+                lf_exit(i, u)
+            if i == 0:
+                m_copy(0)
+            lb(i, nc.vector, SPLIT, N)
+            if not end:
+                bcast(i + 1)
+            q_tile(rC, rS, i, rI, R, "r")
+            interleave(lbI[i], lbN[i], 0, SPLIT)
+            if prev:
+                stage2(i - 1)
+            q_tile(lbC, lbS, i, lbI, N, "lb")
+            stage1(i, lbC, lbS, bwS, h03, "bwS")
+            if not end:
+                r_trans(i + 1)
+            interleave(lfI[i], lfN[i], 0, 256)
+            interleave(lfI[i], lfN[i], 256, 512)
+            if prev:
+                q_p(i - 1, 0, 2)
+            else:
+                q_tile(mC, mS, i, mI, W, "m")
+            q_tile(lfC, lfS, i, lfI, N, "lf")
+            todo = stage1(i, lfC, lfS, fwS, h07, "fwS", "SV" if end else "SS")
+        j = B - 1
+        scale_store(0, j)
         for args in todo:
             exit1(*args)
-        p_exit(k, 0, p_mm(k, 0), "S")
-        p_exit(k, 1, p_mm(k, 1), "S")
-        q_tile(mC, mS, j, mI, W, "m")
         a_add(j, 0)
         a_add(j, 1)
         q_tile(aC, aS, j, aI, R, "a", 0, P)
         q_tile(aC, aS, j, aI, R, "a", P, R)
-        q_p(k, 0, 2)
         pp0 = p_mm(j, 0)
         pp1 = p_mm(j, 1)
+        oo0 = o_mm(j, 0, True)
+        oo1 = o_mm(j, 1, True)
         p_exit(j, 0, pp0, "S")
         p_exit(j, 1, pp1, "V")
-        o_exit(k, 0, o_mm(k, 0), "S")
-        o_exit(k, 1, o_mm(k, 1), "V")
-        o_store(k, 0, 2)
-        q_p(j, 0, 2)
-        o_exit(j, 0, o_mm(j, 0), "S")
+        o_exit(j, 0, oo0, "S")
         o_store(j, 0, 1)
-        o_exit(j, 1, o_mm(j, 1), "V")
+        q_p(j, 0, 2)
+        o_exit(j, 1, oo1, "V")
         o_store(j, 1, 2)
-        scale_store(k, B)
+        scale_store(j, B)

@@ -164,7 +164,8 @@ def tile_dnctemporallinkreadout_x1_kernel(tc, link, w, p, r, g, h, m, out_0, out
                                  func=COPY, scale=g32[:, u:u + 1])
 
         def interleave(dst, src, c0, c1):
-            nc.vector.tensor_copy(out=dst[:, c0:c1, :], in_=src[:, :, c0:c1].rearrange("p u c -> p c u"))
+            nc.vector.tensor_copy(out=dst[:, c0:c1, :].rearrange("p (c i) u -> p c u i", i=4),
+                                  in_=src[:, :, c0:c1].rearrange("p u (c i) -> p c u i", i=4))
 
         def lb_scale(b, c0, c1):
             lbN[b] = work.tile([P, 4, N], BF16, name="lbN", align_bytes=64)
@@ -174,13 +175,15 @@ def tile_dnctemporallinkreadout_x1_kernel(tc, link, w, p, r, g, h, m, out_0, out
         def lb(b, eng, c0, c1):
             lbI[b] = work.tile([P, N, 4], BF16, name="lbI", align_bytes=64)
             eng.tensor_tensor(
-                out=lbI[b][:, c0:c1, :], in0=Q[b][:, :, c0:c1].rearrange("p s c -> p c s"),
-                in1=g_ps[:].unsqueeze(1).to_broadcast([P, c1 - c0, 4]), op=MULT)
+                out=lbI[b][:, c0:c1, :].rearrange("p (c i) s -> p c s i", i=4),
+                in0=Q[b][:, :, c0:c1].rearrange("p s (c i) -> p c s i", i=4),
+                in1=g_ps[:].unsqueeze(1).unsqueeze(3).to_broadcast([P, (c1 - c0) // 4, 4, 4]), op=MULT)
 
         def m_copy(b):
             mI[b] = work.tile([P, W, 4], BF16, name="mI", align_bytes=64)
-            nc.scalar.copy(out=mI[b][:].rearrange("p (t m) j -> p t m j", t=4),
-                           in_=mt[b][:].rearrange("p j (m t) -> p t m j", t=4))
+            for t in range(4):
+                nc.scalar.copy(out=mI[b][:, t * P:(t + 1) * P, :].rearrange("p (m i) j -> p m j i", i=2),
+                               in_=mt[b][:].rearrange("p j (m i t) -> p t m j i", i=2, t=4)[:, t])
 
         def exit1(b, acc, dst, hs, eng, half):
             for i in range(2):
@@ -213,8 +216,9 @@ def tile_dnctemporallinkreadout_x1_kernel(tc, link, w, p, r, g, h, m, out_0, out
                 aI[b] = work.tile([P, R, 4], BF16, name="aI", align_bytes=64)
             ks = slice(c * P, (c + 1) * P)
             nc.vector.tensor_tensor(
-                out=aI[b][:, ks, :], in0=fwS[b][:, :, ks].rearrange("p t k -> p k t"),
-                in1=bwS[b][:, :, ks].rearrange("p t k -> p k t"), op=ADD)
+                out=aI[b][:, ks, :].rearrange("p (k i) t -> p k t i", i=4),
+                in0=fwS[b][:, :, ks].rearrange("p t (k i) -> p k t i", i=4),
+                in1=bwS[b][:, :, ks].rearrange("p t (k i) -> p k t i", i=4), op=ADD)
 
         def p_mm(b, c):
             if c == 0:

@@ -151,10 +151,11 @@ def tile_dnctemporallinkreadout_x1_kernel(tc, link, w, p, r, g, h, m, out_0, out
             nc.gpsimd.affine_select(out=blk, in_=blk, pattern=[[-1, P]], compare_op=mybir.AluOpType.not_equal,
                                     fill=0.0, base=0, channel_multiplier=1)
 
-        def tq(b, u):
-            tr[b, u] = ps_tr.tile([P, 4, P], F32, name="tr_q", tag="tr")
-            for s in range(4):
-                nc.tensor.transpose(tr[b, u][:, s, :], Q[b][:, s, u * P:(u + 1) * P], ident_f[:])
+        def tr_tile(b, u, pool, tag):
+            tr[b, u] = pool.tile([P, 4, P], F32, name="tr_q", tag=tag)
+
+        def tq(b, s, u):
+            nc.tensor.transpose(tr[b, u][:, s, :], Q[b][:, s, u * P:(u + 1) * P], ident_f[:])
 
         def lf_exit(b, u):
             if u == 0:
@@ -194,10 +195,11 @@ def tile_dnctemporallinkreadout_x1_kernel(tc, link, w, p, r, g, h, m, out_0, out
                 else:
                     nc.scalar.activation(out=dst[b][:, t, :], in_=acc[:, i, :], func=COPY, scale=hs[:, t:t + 1])
 
-        def stage1(b, codes, scales, dst, hs, nm, engs="SS"):
-            dst[b] = work.tile([P, 4, R], F32, name=nm, align_bytes=64)
+        def stage1(b, codes, scales, dst, hs, nm, engs="SS", halves=(0, 1)):
+            if halves[0] == 0:
+                dst[b] = work.tile([P, 4, R], F32, name=nm, align_bytes=64)
             todo = []
-            for half in range(2):
+            for half in halves:
                 acc = ps_s1.tile([P, 2, R], F32, name="s1")
                 for i in range(2):
                     t = 2 * half + i
@@ -211,11 +213,11 @@ def tile_dnctemporallinkreadout_x1_kernel(tc, link, w, p, r, g, h, m, out_0, out
                     todo.append((b, acc, dst, hs, "V", half))
             return todo
 
-        def a_add(b, c):
-            if c == 0:
+        def a_add(b, c, eng):
+            if b not in aI:
                 aI[b] = work.tile([P, R, 4], BF16, name="aI", align_bytes=64)
             ks = slice(c * P, (c + 1) * P)
-            nc.vector.tensor_tensor(
+            eng.tensor_tensor(
                 out=aI[b][:, ks, :].rearrange("p (k i) t -> p k t i", i=4),
                 in0=fwS[b][:, :, ks].rearrange("p t (k i) -> p k t i", i=4),
                 in1=bwS[b][:, :, ks].rearrange("p t (k i) -> p k t i", i=4), op=ADD)
@@ -288,14 +290,24 @@ def tile_dnctemporallinkreadout_x1_kernel(tc, link, w, p, r, g, h, m, out_0, out
             v1(i, 1)
             v2(i, 0)
             mask(i, 0)
-            if prev:
+            if end:
+                for u in range(4):
+                    tr_tile(i, u, ps_s2 if u == 3 else ps_tr, "s2" if u == 3 else "tr")
+                    tq(i, 0, u)
+            if prev and not end:
                 m_copy(i)
             v1(i, 2)
             v2(i, 1)
             mask(i, 1)
+            if end:
+                for u in range(4):
+                    tq(i, 1, u)
             v1(i, 3)
             v2(i, 2)
             mask(i, 2)
+            if end:
+                for u in range(4):
+                    tq(i, 2, u)
             if i == 0:
                 r_trans(0)
                 nc.vector.tensor_scalar(out=wm1[1][:], in0=w_ps[1][:], scalar1=-1.0, scalar2=None, op0=ADD)
@@ -304,45 +316,70 @@ def tile_dnctemporallinkreadout_x1_kernel(tc, link, w, p, r, g, h, m, out_0, out
                 nc.vector.tensor_scalar(out=h03[:], in0=h_ps[:], scalar1=0.3, scalar2=None, op0=MULT)
             v2(i, 3)
             mask(i, 3)
+            if prev and not end:
+                a_add(i - 1, 0, nc.vector)
+                a_add(i - 1, 1, nc.vector)
             if prev:
-                a_add(i - 1, 0)
-                a_add(i - 1, 1)
-                q_tile(mC, mS, i, mI, W, "m")
+                q_tile(mC, mS, i - 1, mI, W, "m")
+            if prev and not end:
                 q_tile(aC, aS, i - 1, aI, R, "a")
             for u in range(4):
-                tq(i, u)
+                if end:
+                    tq(i, 3, u)
+                else:
+                    tr_tile(i, u, ps_tr, "tr")
+                    for s in range(4):
+                        tq(i, s, u)
             lb_scale(i, 0, SPLIT)
             for u in range(4):
                 lf_exit(i, u)
+            if i == 0 or end:
+                m_copy(i)
             if i == 0:
-                m_copy(0)
+                q_tile(rC, rS, i, rI, R, "r")
             lb(i, nc.vector, SPLIT, N)
             if not end:
                 bcast(i + 1)
-            q_tile(rC, rS, i, rI, R, "r")
+            if prev and not end:
+                stage2(i - 1)
             interleave(lbI[i], lbN[i], 0, SPLIT)
             if prev:
-                stage2(i - 1)
+                q_tile(rC, rS, i, rI, R, "r")
             q_tile(lbC, lbS, i, lbI, N, "lb")
             stage1(i, lbC, lbS, bwS, h03, "bwS")
             if not end:
                 r_trans(i + 1)
+            else:
+                a_add(i - 1, 0, nc.vector)
+                a_add(i - 1, 1, nc.vector)
+                q_tile(aC, aS, i - 1, aI, R, "a")
+                for c in range(2):
+                    p_exit(i - 1, c, p_mm(i - 1, c), "S")
             interleave(lfI[i], lfN[i], 0, 256)
             interleave(lfI[i], lfN[i], 256, 512)
-            if prev:
-                q_p(i - 1, 0, 2)
+            if not end:
+                if prev:
+                    q_p(i - 1, 0, 2)
+                q_tile(lfC, lfS, i, lfI, N, "lf")
+                stage1(i, lfC, lfS, fwS, h07, "fwS")
             else:
-                q_tile(mC, mS, i, mI, W, "m")
-            q_tile(lfC, lfS, i, lfI, N, "lf")
-            todo = stage1(i, lfC, lfS, fwS, h07, "fwS", "SV" if end else "SS")
-        j = B - 1
-        scale_store(0, j)
+                q_tile(lfC, lfS, i, lfI, N, "lf", 0, 256)
+                stage1(i, lfC, lfS, fwS, h07, "fwS", "SS", (0,))
+                q_tile(lfC, lfS, i, lfI, N, "lf", 256, 512)
+                todo = stage1(i, lfC, lfS, fwS, h07, "fwS", "SV", (1,))
+        j, k = B - 1, B - 2
+        q_tile(mC, mS, j, mI, W, "m")
         for args in todo:
             exit1(*args)
-        a_add(j, 0)
-        a_add(j, 1)
+        for c in range(2):
+            o_exit(k, c, o_mm(k, c), "S")
+        o_store(k, 0, 2)
+        a_add(j, 0, nc.vector)
+        a_add(j, 1, nc.vector)
         q_tile(aC, aS, j, aI, R, "a", 0, P)
         q_tile(aC, aS, j, aI, R, "a", P, R)
+        q_p(k, 0, 2)
+        scale_store(0, j)
         pp0 = p_mm(j, 0)
         pp1 = p_mm(j, 1)
         oo0 = o_mm(j, 0, True)

@@ -282,7 +282,7 @@ def tile_dnctemporallinkreadout_x1_kernel(tc, link, w, p, r, g, h, m, out_0, out
                 o_exit(b, c, o_mm(b, c), "S")
             o_store(b, 0, 2)
 
-        SPLIT = 256
+        SPLIT = 192
         bcast(0)
         for i in range(B):
             prev, end = i > 0, i == B - 1
@@ -375,20 +375,20 @@ def tile_dnctemporallinkreadout_x1_kernel(tc, link, w, p, r, g, h, m, out_0, out
             o_exit(k, c, o_mm(k, c), "S")
         o_store(k, 0, 2)
         a_add(j, 0, nc.vector)
-        a_add(j, 1, nc.vector)
         q_tile(aC, aS, j, aI, R, "a", 0, P)
-        q_tile(aC, aS, j, aI, R, "a", P, R)
+        pp0 = p_mm(j, 0)
+        oo0 = o_mm(j, 0, True)
+        a_add(j, 1, nc.vector)
+        p_exit(j, 0, pp0, "S")
         q_p(k, 0, 2)
         scale_store(0, j)
-        pp0 = p_mm(j, 0)
+        q_tile(aC, aS, j, aI, R, "a", P, R)
         pp1 = p_mm(j, 1)
-        oo0 = o_mm(j, 0, True)
         oo1 = o_mm(j, 1, True)
-        p_exit(j, 0, pp0, "S")
-        p_exit(j, 1, pp1, "V")
         o_exit(j, 0, oo0, "S")
         o_store(j, 0, 1)
-        q_p(j, 0, 2)
-        o_exit(j, 1, oo1, "V")
+        p_exit(j, 1, pp1, "V")
+        o_exit(j, 1, oo1, "S")
         o_store(j, 1, 2)
+        q_p(j, 0, 2)
         scale_store(j, B)

from contextlib import ExitStack

import concourse.mybir as mybir
from concourse.masks import make_identity

FLOPS = 4 * 3 * 2 * 256 * 512 * 512

F32 = mybir.dt.float32
BF16 = mybir.dt.bfloat16
U32 = mybir.dt.uint32
I32 = mybir.dt.int32
U8 = mybir.dt.uint8
FP8X4 = mybir.dt.float8_e4m3fn_x4
ADD = mybir.AluOpType.add
SUB = mybir.AluOpType.subtract
MULT = mybir.AluOpType.mult
COPY = mybir.ActivationFunctionType.Copy

B, N, R, W = 4, 512, 256, 512
P = 128


def tile_dnctemporallinkreadout_x1_kernel(tc, link, w, p, r, g, h, m, out_0, out_1, out_2):
    nc = tc.nc
    with ExitStack() as ctx:
        ctx.enter_context(tc.manual_schedule())
        const = ctx.enter_context(tc.tile_pool(name="const", bufs=1))
        raw = ctx.enter_context(tc.tile_pool(name="raw", bufs=4))
        work = ctx.enter_context(tc.tile_pool(name="work", bufs=2))
        ps_tr = ctx.enter_context(tc.psum_pool(name="ps_tr", bufs=4))
        ps_s1 = ctx.enter_context(tc.psum_pool(name="ps_s1", bufs=2))
        ps_s2 = ctx.enter_context(tc.psum_pool(name="ps_s2", bufs=2))

        w_ps = [const.tile([P, n, 4], BF16, name=f"w_ps{n}", align_bytes=64) for n in (1, B - 1)]
        p_ps = [const.tile([P, n, 4], BF16, name=f"p_ps{n}", align_bytes=64) for n in (1, B - 1)]
        wm1 = [const.tile([P, n, 4], F32, name=f"wm1{n}", align_bytes=64) for n in (1, B - 1)]

        def col(pair, b, s):
            return pair[0][:, 0, s:s + 1] if b == 0 else pair[1][:, b - 1, s:s + 1]
        g_ps = const.tile([P, 4], BF16, name="g_ps", align_bytes=64)
        h_ps = const.tile([P, 4], BF16, name="h_ps", align_bytes=64)
        linkt, rt, mt = {}, {}, {}

        def load_link(b, s0, parts):
            lv = link[b].rearrange("(p s) q -> p s q", s=4)
            for n in parts:
                if n == 4:
                    t = raw.tile([P, n, N], BF16, name="link_all", align_bytes=64)
                else:
                    t = const.tile([P, n, N], BF16, name=f"link_first_{s0}", align_bytes=64)
                nc.sync.dma_start(out=t[:], in_=lv[:, s0:s0 + n, :])
                for j in range(n):
                    linkt[b, s0 + j] = t[:, j, :]
                s0 += n

        def load_r(b):
            t = raw.tile([P, 2, N], BF16, name="r_raw", align_bytes=64)
            nc.sync.dma_start(out=t[:], in_=r[b].rearrange("(c k) j -> k c j", k=P))
            rt[b] = t

        def load_m(b):
            t = raw.tile([P, 4, W], BF16, name="m_raw", align_bytes=64)
            nc.sync.dma_start(out=t[:], in_=m[b].rearrange("(p j) c -> p j c", j=4))
            mt[b] = t

        with nc.allow_non_contiguous_dma(reason="8-byte pieces of the small vectors"):
            wv = w.rearrange("b (p s) -> p b s", s=4)
            pv = p.rearrange("b (p s) -> p b s", s=4)
            nc.scalar.dma_start(out=w_ps[0][:], in_=wv[:, 0:1, :])
            load_link(0, 0, (1,))
            nc.scalar.dma_start(out=p_ps[0][:], in_=pv[:, 0:1, :])
            load_link(0, 1, (1,))
            nc.scalar.dma_start(out=g_ps[:], in_=g.rearrange("(p s) -> p s", s=4))
            load_link(0, 2, (2,))
            nc.scalar.dma_start(out=w_ps[1][:], in_=wv[:, 1:B, :])
            nc.scalar.dma_start(out=p_ps[1][:], in_=pv[:, 1:B, :])
            nc.scalar.dma_start(out=h_ps[:], in_=h.rearrange("(p s) -> p s", s=4))
        load_r(0)
        load_link(1, 0, (4,))
        load_m(0)
        load_r(1)
        load_link(2, 0, (4,))
        load_m(1)
        load_r(2)
        load_link(3, 0, (4,))
        load_r(3)
        load_m(2)
        load_m(3)

        ident_b = const.tile([P, P], BF16, name="ident_b", align_bytes=64)
        ident_f = const.tile([P, P], F32, name="ident_f", align_bytes=64)
        make_identity(nc, ident_b[:])
        make_identity(nc, ident_f[:])
        nc.vector.tensor_scalar(out=wm1[0][:], in0=w_ps[0][:], scalar1=-1.0, scalar2=None, op0=ADD)
        g32 = const.tile([P, 4], F32, name="g32", align_bytes=64)
        h07 = const.tile([P, 4], F32, name="h07", align_bytes=64)
        h03 = const.tile([P, 4], F32, name="h03", align_bytes=64)

        p_codes = const.tile([P, B * R], U32, name="p_codes", align_bytes=64)
        p_scales = const.tile([P, B * R], U8, name="p_scales", align_bytes=64)

        bc, tr, lfN, lbN = {}, {}, {}, {}
        U, Q, lfI, lbI, lfC, lfS, lbC, lbS = {}, {}, {}, {}, {}, {}, {}, {}
        rI, rC, rS, mI, mC, mS = {}, {}, {}, {}, {}, {}
        fwS, bwS, aI, aC, aS, pI, oS = {}, {}, {}, {}, {}, {}, {}

        def bcast(b):
            bc[b] = ps_tr.tile([P, 2, N], BF16, name="bc", tag="tr")
            for i, v in enumerate((w_ps, p_ps)):
                for t in range(4):
                    nc.tensor.transpose(bc[b][:, i, t * P:(t + 1) * P],
                                        col(v, b, t).to_broadcast([P, P]), ident_b[:])

        def r_trans(b):
            t = ps_tr.tile([P, 2, 2, P], F32, name="tr_r", tag="tr")
            for c in range(2):
                words = rt[b][:, c, :].bitcast(F32)
                for u in range(2):
                    nc.tensor.transpose(t[:, c, u, :], words[:, u:2 * P:2], ident_f[:])
            rI[b] = work.tile([P, R, 4], BF16, name="rI", align_bytes=64)
            nc.scalar.copy(
                out=rI[b][:].rearrange("p k t -> p (k t)").bitcast(F32).rearrange("p (c k u) -> p c k u", c=2, u=2),
                in_=t[:].rearrange("p c u k -> p c k u"))

        def quant(src, cols, codes, scales):
            nc.vector.quantize_mx(out=codes.bitcast(FP8X4), scales=scales, in_=src)

        def q_tile(store_c, store_s, b, src, cols, nm, n0=0, n1=None):
            n1 = cols if n1 is None else n1
            if n0 == 0:
                store_c[b] = work.tile([P, cols], U32, name=nm + "C", align_bytes=64)
                store_s[b] = work.tile([P, cols], U8, name=nm + "S", align_bytes=64)
            quant(src[b][:, n0:n1, :].rearrange("p c s -> p (c s)"), cols, store_c[b][:, n0:n1], store_s[b][:, n0:n1])

        def v1(b, s):
            if s == 0:
                Q[b] = work.tile([P, 4, N], F32, name="Q", align_bytes=64)
            U[b, s] = work.tile([P, N], F32, name="U", bufs=4, align_bytes=64)
            nc.vector.scalar_tensor_tensor(
                out=U[b, s][:].rearrange("p (u m) -> p u m", u=4),
                in0=bc[b][:, 0, :].rearrange("p (u m) -> p u m", u=4), scalar=col(wm1, b, s),
                in1=linkt[b, s].rearrange("p (m u) -> p u m", u=4), op0=ADD, op1=MULT)

        def v2(b, s):
            nc.vector.scalar_tensor_tensor(
                out=Q[b][:, s, :], in0=bc[b][:, 1, :], scalar=col(w_ps, b, s),
                in1=U[b, s][:], op0=MULT, op1=SUB)

        def mask(b, s):
            blk = Q[b][:, s, s * P:(s + 1) * P]
            nc.gpsimd.affine_select(out=blk, in_=blk, pattern=[[-1, P]], compare_op=mybir.AluOpType.not_equal,
                                    fill=0.0, base=0, channel_multiplier=1)

        def tr_tile(b, u, pool, tag):
            tr[b, u] = pool.tile([P, 4, P], F32, name="tr_q", tag=tag)

        def tq(b, s, u):
            nc.tensor.transpose(tr[b, u][:, s, :], Q[b][:, s, u * P:(u + 1) * P], ident_f[:])

        def lf_exit(b, u):
            if u == 0:
                lfN[b] = work.tile([P, 4, N], BF16, name="lfN", align_bytes=64)
                lfI[b] = work.tile([P, N, 4], BF16, name="lfI", align_bytes=64)
            nc.scalar.activation(out=lfN[b][:, u, :], in_=tr[b, u][:].rearrange("p s k -> p (s k)"),
                                 func=COPY, scale=g32[:, u:u + 1])

        def interleave(dst, src, c0, c1):
            nc.vector.tensor_copy(out=dst[:, c0:c1, :].rearrange("p (c i) u -> p c u i", i=4),
                                  in_=src[:, :, c0:c1].rearrange("p u (c i) -> p c u i", i=4))

        def lb_scale(b, c0, c1):
            lbN[b] = work.tile([P, 4, N], BF16, name="lbN", align_bytes=64)
            for s in range(4):
                nc.scalar.activation(out=lbN[b][:, s, c0:c1], in_=Q[b][:, s, c0:c1], func=COPY, scale=g32[:, s:s + 1])

        def lb(b, eng, c0, c1):
            lbI[b] = work.tile([P, N, 4], BF16, name="lbI", align_bytes=64)
            eng.tensor_tensor(
                out=lbI[b][:, c0:c1, :].rearrange("p (c i) s -> p c s i", i=4),
                in0=Q[b][:, :, c0:c1].rearrange("p s (c i) -> p c s i", i=4),
                in1=g_ps[:].unsqueeze(1).unsqueeze(3).to_broadcast([P, (c1 - c0) // 4, 4, 4]), op=MULT)

        def m_copy(b):
            mI[b] = work.tile([P, W, 4], BF16, name="mI", align_bytes=64)
            for t in range(4):
                nc.scalar.copy(out=mI[b][:, t * P:(t + 1) * P, :].rearrange("p (m i) j -> p m j i", i=2),
                               in_=mt[b][:].rearrange("p j (m i t) -> p t m j i", i=2, t=4)[:, t])

        def exit1(b, acc, dst, hs, eng, half):
            for i in range(2):
                t = 2 * half + i
                if eng == "V":
                    nc.vector.tensor_scalar(out=dst[b][:, t, :], in0=acc[:, i, :], scalar1=hs[:, t:t + 1],
                                            scalar2=None, op0=MULT)
                else:
                    nc.scalar.activation(out=dst[b][:, t, :], in_=acc[:, i, :], func=COPY, scale=hs[:, t:t + 1])

        def stage1(b, codes, scales, dst, hs, nm, engs="SS", halves=(0, 1)):
            if halves[0] == 0:
                dst[b] = work.tile([P, 4, R], F32, name=nm, align_bytes=64)
            todo = []
            for half in halves:
                acc = ps_s1.tile([P, 2, R], F32, name="s1")
                for i in range(2):
                    t = 2 * half + i
                    nc.tensor.matmul_mx(
                        out=acc[:, i, :], lhsT=codes[b][:, t * P:(t + 1) * P].bitcast(FP8X4),
                        lhsT_scale=scales[b][:, t * P:(t + 1) * P],
                        rhs=rC[b][:].bitcast(FP8X4), rhs_scale=rS[b][:], start=True, stop=True)
                if engs[half] == "S":
                    exit1(b, acc, dst, hs, "S", half)
                else:
                    todo.append((b, acc, dst, hs, "V", half))
            return todo

        def a_add(b, c, eng):
            if b not in aI:
                aI[b] = work.tile([P, R, 4], BF16, name="aI", align_bytes=64)
            ks = slice(c * P, (c + 1) * P)
            eng.tensor_tensor(
                out=aI[b][:, ks, :].rearrange("p (k i) t -> p k t i", i=4),
                in0=fwS[b][:, :, ks].rearrange("p t (k i) -> p k t i", i=4),
                in1=bwS[b][:, :, ks].rearrange("p t (k i) -> p k t i", i=4), op=ADD)

        def p_mm(b, c):
            if c == 0:
                pI[b] = work.tile([P, R, 4], BF16, name="pI", align_bytes=64)
            ks = slice(c * P, (c + 1) * P)
            pp = ps_s2.tile([P, 4, P], F32, name="pp", tag="s2")
            for t in range(4):
                nc.tensor.matmul_mx(
                    out=pp[:, t, :], lhsT=mC[b][:, t * P:(t + 1) * P].bitcast(FP8X4),
                    lhsT_scale=mS[b][:, t * P:(t + 1) * P],
                    rhs=aC[b][:, ks].bitcast(FP8X4), rhs_scale=aS[b][:, ks], start=True, stop=True)
            return pp

        def p_exit(b, c, pp, eng):
            ks = slice(c * P, (c + 1) * P)
            if eng == "V":
                nc.vector.tensor_copy(out=pI[b][:, ks, :], in_=pp[:].rearrange("p t k -> p k t"))
            else:
                nc.scalar.copy(out=pI[b][:, ks, :], in_=pp[:].rearrange("p t k -> p k t"))

        def o_mm(b, c, early=False):
            if c == 0:
                oS[b] = work.tile([P, 2, W], F32, name="oS", align_bytes=64)
            ks = slice(c * P, (c + 1) * P)
            pool, tag = (ps_tr, "tr") if early else (ps_s2, "s2")
            oo = pool.tile([P, W], F32, name="oo", tag=tag)
            nc.tensor.matmul_mx(
                out=oo[:], lhsT=aC[b][:, ks].bitcast(FP8X4), lhsT_scale=aS[b][:, ks],
                rhs=mC[b][:].bitcast(FP8X4), rhs_scale=mS[b][:], start=True, stop=True)
            return oo

        def o_exit(b, c, oo, eng):
            dst = oS[b][:, c, :].rearrange("p (m t) -> p m t", t=4)
            src = oo[:].rearrange("p (t m) -> p m t", t=4)
            if eng == "V":
                nc.vector.tensor_copy(out=dst, in_=src)
            else:
                nc.scalar.copy(out=dst, in_=src)

        def o_store(b, c0, c1):
            nc.sync.dma_start(out=out_0[b].rearrange("(c k) n -> k c n", k=P)[:, c0:c1, :], in_=oS[b][:, c0:c1, :])

        def q_p(b, c0, c1):
            ms = slice(b * R + c0 * P, b * R + c1 * P)
            quant(pI[b][:, c0 * P:c1 * P, :].rearrange("p c s -> p (c s)"), R, p_codes[:, ms], p_scales[:, ms])
            nc.sync.dma_start(out=out_1[0, :, ms, :].rearrange("p k t -> p (k t)").bitcast(I32),
                              in_=p_codes[:, ms].bitcast(I32))

        def scale_store(b0, b1):
            ms = slice(b0 * R, b1 * R)
            for q in range(4):
                nc.sync.dma_start(out=out_2[0, 4 * q:4 * q + 4, ms].bitcast(I32),
                                  in_=p_scales[32 * q:32 * q + 4, ms].bitcast(I32))

        def stage2(b):
            for c in range(2):
                p_exit(b, c, p_mm(b, c), "S")
            for c in range(2):
                o_exit(b, c, o_mm(b, c), "S")
            o_store(b, 0, 2)

        SPLIT = 192
        bcast(0)
        for i in range(B):
            prev, end = i > 0, i == B - 1
            v1(i, 0)
            v1(i, 1)
            v2(i, 0)
            mask(i, 0)
            if end:
                for u in range(4):
                    tr_tile(i, u, ps_s2 if u == 3 else ps_tr, "s2" if u == 3 else "tr")
                    tq(i, 0, u)
            if prev and not end:
                m_copy(i)
            v1(i, 2)
            v2(i, 1)
            mask(i, 1)
            if end:
                for u in range(4):
                    tq(i, 1, u)
            v1(i, 3)
            v2(i, 2)
            mask(i, 2)
            if end:
                for u in range(4):
                    tq(i, 2, u)
            if i == 0:
                r_trans(0)
                nc.vector.tensor_scalar(out=wm1[1][:], in0=w_ps[1][:], scalar1=-1.0, scalar2=None, op0=ADD)
                nc.vector.tensor_scalar(out=g32[:], in0=g_ps[:], scalar1=1.0, scalar2=None, op0=MULT)
                nc.vector.tensor_scalar(out=h07[:], in0=h_ps[:], scalar1=0.7, scalar2=None, op0=MULT)
                nc.vector.tensor_scalar(out=h03[:], in0=h_ps[:], scalar1=0.3, scalar2=None, op0=MULT)
            v2(i, 3)
            mask(i, 3)
            if prev and not end:
                a_add(i - 1, 0, nc.vector)
                a_add(i - 1, 1, nc.vector)
            if prev:
                q_tile(mC, mS, i - 1, mI, W, "m")
            if prev and not end:
                q_tile(aC, aS, i - 1, aI, R, "a")
            for u in range(4):
                if end:
                    tq(i, 3, u)
                else:
                    tr_tile(i, u, ps_tr, "tr")
                    for s in range(4):
                        tq(i, s, u)
            lb_scale(i, 0, SPLIT)
            for u in range(4):
                lf_exit(i, u)
            if i == 0 or end:
                m_copy(i)
            if i == 0:
                q_tile(rC, rS, i, rI, R, "r")
            lb(i, nc.vector, SPLIT, N)
            if not end:
                bcast(i + 1)
            if prev and not end:
                stage2(i - 1)
            interleave(lbI[i], lbN[i], 0, SPLIT)
            if prev:
                q_tile(rC, rS, i, rI, R, "r")
            q_tile(lbC, lbS, i, lbI, N, "lb")
            stage1(i, lbC, lbS, bwS, h03, "bwS")
            if not end:
                r_trans(i + 1)
            else:
                a_add(i - 1, 0, nc.vector)
                a_add(i - 1, 1, nc.vector)
                q_tile(aC, aS, i - 1, aI, R, "a")
                for c in range(2):
                    p_exit(i - 1, c, p_mm(i - 1, c), "S")
            interleave(lfI[i], lfN[i], 0, 256)
            interleave(lfI[i], lfN[i], 256, 512)
            if not end:
                if prev:
                    q_p(i - 1, 0, 2)
                q_tile(lfC, lfS, i, lfI, N, "lf")
                stage1(i, lfC, lfS, fwS, h07, "fwS")
            else:
                q_tile(lfC, lfS, i, lfI, N, "lf", 0, 256)
                stage1(i, lfC, lfS, fwS, h07, "fwS", "SS", (0,))
                q_tile(lfC, lfS, i, lfI, N, "lf", 256, 512)
                todo = stage1(i, lfC, lfS, fwS, h07, "fwS", "SV", (1,))
        j, k = B - 1, B - 2
        q_tile(mC, mS, j, mI, W, "m")
        for args in todo:
            exit1(*args)
        for c in range(2):
            o_exit(k, c, o_mm(k, c), "S")
        o_store(k, 0, 2)
        a_add(j, 0, nc.vector)
        q_tile(aC, aS, j, aI, R, "a", 0, P)
        pp0 = p_mm(j, 0)
        oo0 = o_mm(j, 0, True)
        a_add(j, 1, nc.vector)
        p_exit(j, 0, pp0, "S")
        q_p(k, 0, 2)
        scale_store(0, j)
        q_tile(aC, aS, j, aI, R, "a", P, R)
        pp1 = p_mm(j, 1)
        oo1 = o_mm(j, 1, True)
        o_exit(j, 0, oo0, "S")
        o_store(j, 0, 1)
        p_exit(j, 1, pp1, "V")
        o_exit(j, 1, oo1, "S")
        o_store(j, 1, 2)
        q_p(j, 0, 2)
        scale_store(j, B)
